import numpy as np
import ml_dtypes


def mxq(x, axis, fmt="e4m3"):
    dtype, down = {"e4m3": (ml_dtypes.float8_e4m3fn, 7), "e5m2": (ml_dtypes.float8_e5m2, 14)}[fmt]
    v = np.moveaxis(np.asarray(x, np.float32).astype(ml_dtypes.bfloat16).astype(np.float64), axis, -1)
    blocks = v.reshape(v.shape[:-1] + (-1, 32))
    amax = np.abs(blocks).max(-1, keepdims=True)
    byte = np.maximum(np.where(amax > 0, np.frexp(amax)[1] - 1 + 127, 0) - down, 1)
    scale = np.exp2(byte - 127.0)
    codes = (blocks / scale).astype(np.float32).astype(dtype).astype(np.float64)
    return np.moveaxis((codes * scale).reshape(v.shape), -1, axis)


WIDE = False


def mx_kscale(k):
    if not WIDE:
        return np.ones(k)
    levels = np.array([10, -10, 5, -5, 0])
    if k % 512:
        return np.exp2(np.random.permutation(np.resize(levels, k // 32))).repeat(32)
    a = np.empty((k // 512, 16))
    for p in range(k // 512):
        a[p, :8] = np.random.permutation(np.resize(levels, 8))
        for g in range(8):
            far = levels[np.abs(levels - a[p, g]) >= 10]
            a[p, g + 8] = far[np.random.randint(len(far))]
    return np.exp2(a.ravel()).repeat(32)


def f64(x):
    return np.asarray(x).astype(np.float64)


def striped(idx):
    return np.tile(idx.reshape(-1, 16).T, (8, 1)).astype(np.uint16)


def unstriped(offs):
    return offs[:16].T.reshape(-1).astype(np.int64)


def pack_weight(w):
    k, n = w.shape
    w = f64(np.asarray(w, np.float32).astype(ml_dtypes.bfloat16)).reshape(k // 32, 32, n)
    amax = np.abs(w).max(1)
    byte = np.clip(np.where(amax > 0, np.frexp(amax)[1] - 1 + 127 - 7, 1), 1, 254)
    scaled = (w * np.exp2(127.0 - byte)[:, None, :]).reshape(k, n).astype(np.float32)
    words = np.ascontiguousarray(scaled.reshape(k // 512, 128, 4, n).transpose(0, 1, 3, 2)).astype(ml_dtypes.float8_e4m3fn).view(np.uint8)
    return words, np.ascontiguousarray(byte.astype(np.uint8).reshape(k // 512, 16, n))


def unpack_weight(words, scales):
    g, p, n, _ = words.shape
    vals = np.ascontiguousarray(words).view(ml_dtypes.float8_e4m3fn).astype(np.float64) * np.repeat(np.exp2(scales.astype(np.float64) - 127.0), 8, axis=1)[..., None]
    return vals.transpose(0, 1, 3, 2).reshape(g * 512, n)


K, T, S, N, H = 1024, 2048, 512, 128, 512


def setup_inputs():
    n = np.random.standard_normal
    s = mx_kscale(K)[:, None]
    u = mx_kscale(H)
    packed_xT = pack_weight(n((K, T)) * s)
    return {
        "x_words": packed_xT[0],
        "x_scales": packed_xT[1],
        "w1": (n((K, H)) / np.sqrt(K) / s).astype(np.float32),
        "w2": (n((K, H)) / np.sqrt(K) / s).astype(np.float32),
        "x1": (np.random.uniform(0.1, 0.9, (H, S))).astype(np.float32),
        "unit": (np.random.uniform(0.6, 1.4, (H, 1)) * u[:, None]).astype(np.float32),
        "w3": (n((H, N)) / np.sqrt(H) / u[:, None]).astype(np.float32),
        "offs": striped(np.random.permutation(T)[:S]),
        "cmp": striped(np.random.permutation(S)),
    }


def reference(x_words, x_scales, w1, w2, x1, unit, w3, offs, cmp):
    x2 = -1.0 * f64(x1) + 1.0
    xq = unpack_weight(x_words, x_scales)[:, unstriped(offs)]
    tau = mxq(f64(w2), 0, "e4m3").T @ xq
    tau1 = np.tanh(tau)
    gam = np.exp(-0.7 * tau1)
    den1 = f64(x1) + x2 * gam
    r1 = gam / den1
    gg2 = mxq(f64(w1), 0, "e4m3").T @ xq
    gam2 = np.exp(-0.7 * np.tanh(gg2))
    den2 = x2 + f64(x1) * gam2
    lga = ((x2) ** 2) * (tau1 * ((r1) ** 2) + gam2 / ((den2) ** 2))
    gex = (f64(x1) * x2) * ((tau1 * gam) / den1 + gam2 / den2)
    gc = gex[:, unstriped(cmp)]
    hid = f64(unit) * (lga - gc)
    return mxq(f64(w3), 0, "e4m3").T @ mxq(hid, 0, "e4m3")

@@ -1,0 +1,349 @@
+from contextlib import ExitStack
+
+import concourse.mybir as mybir
+from concourse.masks import make_identity
+
+K, T, S, N, H = 1024, 2048, 512, 128, 512
+FLOPS = 2 * 2 * K * H * S + 2 * H * N * S
+
+F32 = mybir.dt.float32
+BF16 = mybir.dt.bfloat16
+I32 = mybir.dt.int32
+U32 = mybir.dt.uint32
+U16 = mybir.dt.uint16
+U8 = mybir.dt.uint8
+FP8X4 = mybir.dt.float8_e4m3fn_x4
+ACT = mybir.ActivationFunctionType
+ALU = mybir.AluOpType
+
+P = 128
+PACK = 4
+PASSES = K // (P * PACK)
+CHUNKS = S // P
+ALPHA = 0.7
+TINY = 2.0 ** -60
+HALF_S = S // 2
+HALF_H = H // 2
+HALF_P = P // 2
+CAST_STEP = 32
+
+
+def tile_picked_ynrtlg_lng_p_kernel(
+    tc, x_words, x_scales, w1, w2, x1, unit, w3, offs, cmp, out
+):
+    nc = tc.nc
+    with ExitStack() as ctx:
+        keep = ctx.enter_context(tc.tile_pool(name="keep", bufs=1))
+        work = ctx.enter_context(tc.tile_pool(name="work", bufs=3))
+        psum = ctx.enter_context(tc.psum_pool(name="psum", bufs=4))
+
+        offs_sb = keep.tile([P, S // 16], U16, name="offs_sb")
+        cmp_sb = keep.tile([P, S // 16], U16, name="cmp_sb")
+        x1_sb = [keep.tile([P, 2, S], F32, name="x1_%d" % i) for i in range(2)]
+        table_scales = keep.tile([P, T], U8, name="table_scales", align_bytes=64)
+        table_words = [keep.tile([P, T], I32, name="table_words%d" % g, align_bytes=64) for g in range(PASSES)]
+        w3_raw = keep.tile([P, PACK, N], F32, name="w3_raw")
+        unit_sb = keep.tile([P, PACK], F32, name="unit_sb")
+        ident = keep.tile([P, P], F32, name="ident")
+
+        raw = {}
+
+        def load_weight(key, w, g, first, width):
+            raw[key] = keep.tile([P, PACK, width], F32, name="raw_" + key)
+            rows = w[g * P * PACK : (g + 1) * P * PACK, first : first + width]
+            nc.sync.dma_start(out=raw[key][:], in_=rows.rearrange("(p j) h -> p j h", j=PACK))
+
+        def load_words(g):
+            nc.sync.dma_start(
+                out=table_words[g][:], in_=x_words[g].rearrange("p n t -> p (n t)").bitcast(I32)
+            )
+
+        x1_dealt = x1.rearrange("(p t) s -> p t s", t=PACK)
+        nc.vector.memset(table_scales[:].bitcast(I32), 0)
+        make_identity(nc, ident[:])
+        nc.sync.dma_start(offs_sb[:], offs)
+        nc.sync.dma_start(out=x1_sb[0][:], in_=x1_dealt[:, 0:2, :])
+        for q in range(4):
+            nc.sync.dma_start(
+                out=table_scales[32 * q : 32 * q + 4 * PASSES, :].bitcast(I32),
+                in_=x_scales[:, 4 * q : 4 * q + 4, :].bitcast(I32),
+            )
+        nc.sync.dma_start(out=x1_sb[1][:], in_=x1_dealt[:, 2:4, :])
+        load_words(0)
+        load_weight("w2_00", w2, 0, 0, HALF_H)
+        load_words(1)
+        load_weight("w2_01", w2, 1, 0, HALF_H)
+        load_weight("w2_10", w2, 0, HALF_H, HALF_H)
+        load_weight("w2_11", w2, 1, HALF_H, HALF_H)
+        load_weight("w1_0", w1, 0, 0, H)
+        load_weight("w1_1", w1, 1, 0, H)
+        nc.sync.dma_start(out=unit_sb[:], in_=unit.rearrange("(p t) o -> p (t o)", t=PACK))
+        nc.sync.dma_start(cmp_sb[:], cmp)
+        nc.sync.dma_start(out=w3_raw[:], in_=w3.rearrange("(p j) n -> p j n", j=PACK))
+
+        def x1_rows(t):
+            return x1_sb[t // 2][:, t % 2, :]
+
+        def flipped_tile(name):
+            return keep.tile([P, CHUNKS, PACK, P], F32, name=name)
+
+        def by_slot(tile, t):
+            return tile[:, :, t, :]
+
+        def by_half(tile, half, pair):
+            rows = tile[:].rearrange("s c t p -> s (c t) p")
+            return rows[:, 8 * pair : 8 * pair + 8, half * HALF_P : (half + 1) * HALF_P]
+
+        logit = flipped_tile("logit")
+        logs = []
+        for t in range(PACK):
+            bank = psum.tile([P, S], F32, name="bank_a", bufs=4)
+            for c in range(CHUNKS):
+                cols = slice(c * P, (c + 1) * P)
+                nc.tensor.transpose(bank[:, cols], x1_rows(t)[:, cols], ident[:])
+            ln1 = keep.tile([P, CHUNKS, P], F32, name="ln1_%d" % t)
+            ln2 = keep.tile([P, CHUNKS, P], F32, name="ln2_%d" % t)
+            view = bank[:].rearrange("s (c p) -> s c p", p=P)
+            nc.scalar.activation(out=ln1[:], in_=view, func=ACT.Ln, bias=TINY)
+            nc.scalar.activation(out=ln2[:], in_=view, func=ACT.Ln, scale=-1.0, bias=1.0)
+            logs.append((ln1, ln2))
+
+        picked_scales = keep.tile([P, S], U8, name="picked_scales", align_bytes=64)
+        picked_words = [keep.tile([P, S], U32, name="picked_words%d" % g, align_bytes=64) for g in range(PASSES)]
+
+        def gather_words(g):
+            nc.vector.tensor_copy(picked_words[g][:], table_words[g][:].bitcast(U32).indirect(offs_sb[:]))
+
+        rounded = {}
+        codes = {}
+        scales = {}
+
+        def cast_weight(key, vector_m):
+            width = raw[key].shape[2]
+            rounded[key] = keep.tile([P, PACK * width], BF16, name="bf_" + key, align_bytes=64)
+            src = raw[key][:].rearrange("p j (m t) -> p m t j", t=PACK)
+            dst = rounded[key][:].rearrange("p (t m j) -> p m t j", t=PACK, j=PACK)
+            count = width // PACK
+            if vector_m > 0:
+                nc.vector.tensor_copy(out=dst[:, 0:vector_m], in_=src[:, 0:vector_m])
+            for m in range(vector_m, count, CAST_STEP):
+                nc.scalar.copy(out=dst[:, m : m + CAST_STEP], in_=src[:, m : m + CAST_STEP])
+
+        def quantize_weight(key):
+            width = raw[key].shape[2]
+            codes[key] = keep.tile([P, width], U32, name="codes_" + key, align_bytes=64)
+            scales[key] = keep.tile([P, width], U8, name="scales_" + key, align_bytes=64)
+            nc.vector.quantize_mx(out=codes[key][:].bitcast(FP8X4), scales=scales[key][:], in_=rounded[key][:])
+
+        def product(keys, hcols, chunks):
+            width = hcols.stop - hcols.start
+            bank = psum.tile([P, S], F32, name="bank_a", bufs=4)
+            for i, c in enumerate(chunks):
+                cols = slice(c * P, (c + 1) * P)
+                for g in range(PASSES):
+                    nc.tensor.matmul_mx(
+                        out=bank[:, i * width : (i + 1) * width],
+                        lhsT=picked_words[g][:, cols].bitcast(FP8X4),
+                        lhsT_scale=picked_scales[4 * g : P, cols],
+                        rhs=codes[keys[g]][:, hcols].bitcast(FP8X4),
+                        rhs_scale=scales[keys[g]][:, hcols],
+                        start=(g == 0),
+                        stop=(g == PASSES - 1),
+                    )
+            return bank
+
+        def local_terms(bounded, factor, odds, first, second):
+            run = odds.shape[2]
+            z = work.tile([P, S], F32, name="z")
+            nc.vector.scalar_tensor_tensor(
+                out=z[:].rearrange("s (a b) -> s a b", b=run),
+                in0=bounded[:].rearrange("s (a b) -> s a b", b=run),
+                scalar=ALPHA,
+                in1=odds,
+                op0=ALU.mult,
+                op1=ALU.add,
+            )
+            th = work.tile([P, S], F32, name="th")
+            nc.scalar.activation(out=th[:], in_=z[:], func=ACT.Tanh, scale=-0.5)
+            th_view = th[:].rearrange("s (a b) -> s a b", b=run)
+            nc.vector.scalar_tensor_tensor(
+                out=first,
+                in0=th_view,
+                scalar=1.0,
+                in1=factor[:].rearrange("s (a b) -> s a b", b=run),
+                op0=ALU.add,
+                op1=ALU.mult,
+            )
+            nc.vector.scalar_tensor_tensor(
+                out=second, in0=th_view, scalar=1.0, in1=first, op0=ALU.add, op1=ALU.mult
+            )
+
+        def flip(bank, blocks, opens):
+            for c in range(CHUNKS):
+                nc.tensor.matmul(
+                    bank[:, c * P : (c + 1) * P],
+                    blocks[:, c, :],
+                    ident[:],
+                    start=(opens and c == 0),
+                    stop=(not opens and c == CHUNKS - 1),
+                    is_transpose=True,
+                )
+
+        nc.vector.tensor_copy(picked_scales[:], table_scales[:].indirect(offs_sb[:]))
+        gather_words(0)
+        cast_weight("w2_00", 64)
+        gather_words(1)
+        quantize_weight("w2_00")
+        cast_weight("w2_01", 64)
+        quantize_weight("w2_01")
+        for t in range(PACK):
+            nc.vector.tensor_tensor(out=by_slot(logit, t), in0=logs[t][0][:], in1=logs[t][1][:], op=ALU.subtract)
+
+        first1 = flipped_tile("first1")
+        second1 = flipped_tile("second1")
+
+        bounded1 = {}
+
+        def start1(half, pair):
+            bank = product(["w2_%d%d" % (half, g) for g in range(PASSES)], slice(0, HALF_H), [2 * pair, 2 * pair + 1])
+            bounded1[half, pair] = work.tile([P, S], F32, name="bounded")
+            nc.scalar.activation(out=bounded1[half, pair][:], in_=bank[:], func=ACT.Tanh)
+
+        def terms1(half, pair):
+            tau1 = bounded1[half, pair]
+            local_terms(
+                tau1, tau1, by_half(logit, half, pair), by_half(first1, half, pair), by_half(second1, half, pair)
+            )
+
+        start1(0, 0)
+        start1(0, 1)
+        cast_weight("w2_10", 64)
+        cast_weight("w2_11", 64)
+        quantize_weight("w2_10")
+        quantize_weight("w2_11")
+        cast_weight("w1_1", 64)
+        cast_weight("w1_0", 64)
+        quantize_weight("w1_0")
+        quantize_weight("w1_1")
+        terms1(0, 0)
+        start1(1, 0)
+        terms1(0, 1)
+        start1(1, 1)
+        terms1(1, 0)
+        terms1(1, 1)
+
+        unit_half = keep.tile([P, PACK], F32, name="unit_half")
+        unit_quarter = keep.tile([P, PACK], F32, name="unit_quarter")
+        nc.gpsimd.tensor_scalar(unit_half[:], unit_sb[:], 0.5, 0.0, ALU.mult, ALU.add)
+        nc.gpsimd.tensor_scalar(unit_quarter[:], unit_sb[:], 0.25, 0.0, ALU.mult, ALU.add)
+
+        w3_bf = keep.tile([P, N, PACK], BF16, name="w3_bf", align_bytes=64)
+        w3_codes = keep.tile([P, N], U32, name="w3_codes", align_bytes=64)
+        w3_scales = keep.tile([P, N], U8, name="w3_scales", align_bytes=64)
+        hid_rows = keep.tile([P, PACK, S], BF16, name="hid_rows")
+
+        sums = {}
+        bounded2 = {}
+        gam2 = {}
+
+        def open_sums(t):
+            sums[t] = [psum.tile([P, S], F32, name="bank_b", bufs=4) for i in range(2)]
+            flip(sums[t][0], by_slot(first1, t), True)
+            flip(sums[t][1], by_slot(second1, t), True)
+
+        def start2(t):
+            bank = product(["w1_0", "w1_1"], slice(t * P, (t + 1) * P), range(CHUNKS))
+            bounded2[t] = work.tile([P, S], F32, name="bounded")
+            gam2[t] = work.tile([P, S], F32, name="gam2")
+            nc.scalar.activation(out=bounded2[t][:], in_=bank[:], func=ACT.Tanh, scale=-1.0)
+            nc.scalar.activation(out=gam2[t][:], in_=bounded2[t][:], func=ACT.Exp, scale=ALPHA)
+
+        def terms2(t):
+            first2 = work.tile([P, CHUNKS, P], F32, name="first2")
+            second2 = work.tile([P, CHUNKS, P], F32, name="second2")
+            local_terms(bounded2[t], gam2[t], by_slot(logit, t), first2[:], second2[:])
+            flip(sums[t][0], first2[:], False)
+            flip(sums[t][1], second2[:], False)
+
+        def finish(t):
+            gex = work.tile([P, S], F32, name="gex")
+            nc.vector.scalar_tensor_tensor(
+                out=gex[:], in0=sums[t][0][:], scalar=unit_half[:, t : t + 1], in1=x1_rows(t), op0=ALU.mult, op1=ALU.mult
+            )
+            other = work.tile([P, S], F32, name="other")
+            for h in range(2):
+                cols = slice(h * HALF_S, (h + 1) * HALF_S)
+                named = gex[:].indirect(cmp_sb[:, h * HALF_S // 16 : (h + 1) * HALF_S // 16])
+                if t == PACK - 1 and h == 0:
+                    nc.vector.tensor_copy(other[:, cols], named)
+                else:
+                    nc.scalar.activation(out=other[:, cols], in_=named, func=ACT.Copy)
+            parts = 2 if t == PACK - 1 else 1
+            for h in range(parts):
+                cols = slice(h * S // parts, (h + 1) * S // parts)
+                nc.vector.scalar_tensor_tensor(
+                    out=hid_rows[:, t, cols],
+                    in0=sums[t][1][:, cols],
+                    scalar=unit_quarter[:, t : t + 1],
+                    in1=other[:, cols],
+                    op0=ALU.mult,
+                    op1=ALU.subtract,
+                )
+
+        def cast_w3():
+            nc.scalar.copy(
+                out=w3_bf[:].rearrange("p (c i) j -> p c j i", i=4),
+                in_=w3_raw[:].rearrange("p j (c i) -> p c j i", i=4),
+            )
+
+        def quantize_w3():
+            nc.vector.quantize_mx(
+                out=w3_codes[:].bitcast(FP8X4), scales=w3_scales[:], in_=w3_bf[:].rearrange("p n j -> p (n j)")
+            )
+
+        start2(0)
+        start2(1)
+        open_sums(0)
+        terms2(0)
+        start2(2)
+        open_sums(1)
+        terms2(1)
+        start2(3)
+        open_sums(2)
+        finish(0)
+        terms2(2)
+        cast_w3()
+        finish(1)
+        open_sums(3)
+        terms2(3)
+        quantize_w3()
+        finish(2)
+        finish(3)
+
+        for h in range(2):
+            hid_bf = work.tile([P, HALF_S, PACK], BF16, name="hid_bf", align_bytes=64)
+            weave = nc.vector.tensor_copy if h == 0 else nc.scalar.copy
+            weave(
+                out=hid_bf[:].rearrange("p (c i) t -> p c t i", i=4),
+                in_=hid_rows[:, :, h * HALF_S : (h + 1) * HALF_S].rearrange("p t (c i) -> p c t i", i=4),
+            )
+            hid_codes = work.tile([P, HALF_S], U32, name="hid_codes", align_bytes=64)
+            hid_scales = work.tile([P, HALF_S], U8, name="hid_scales", align_bytes=64)
+            nc.vector.quantize_mx(
+                out=hid_codes[:].bitcast(FP8X4),
+                scales=hid_scales[:],
+                in_=hid_bf[:].rearrange("p s t -> p (s t)"),
+            )
+            bank = psum.tile([P, HALF_S], F32, name="bank_a", bufs=4)
+            nc.tensor.matmul_mx(
+                out=bank[:],
+                lhsT=w3_codes[:].bitcast(FP8X4),
+                lhsT_scale=w3_scales[:],
+                rhs=hid_codes[:].bitcast(FP8X4),
+                rhs_scale=hid_scales[:],
+                start=True,
+                stop=True,
+            )
+            result = work.tile([P, HALF_S], F32, name="result")
+            nc.scalar.copy(out=result[:], in_=bank[:])
+            nc.sync.dma_start(out=out[:, h * HALF_S : (h + 1) * HALF_S], in_=result[:])

@@ -25,7 +25,7 @@ TINY = 2.0 ** -60
 HALF_S = S // 2
 HALF_H = H // 2
 HALF_P = P // 2
-CAST_STEP = 32
+CAST_STEP = 128
 
 
 def tile_picked_ynrtlg_lng_p_kernel(
@@ -34,7 +34,7 @@ def tile_picked_ynrtlg_lng_p_kernel(
     nc = tc.nc
     with ExitStack() as ctx:
         keep = ctx.enter_context(tc.tile_pool(name="keep", bufs=1))
-        work = ctx.enter_context(tc.tile_pool(name="work", bufs=3))
+        work = ctx.enter_context(tc.tile_pool(name="work", bufs=4))
         psum = ctx.enter_context(tc.psum_pool(name="psum", bufs=4))
 
         offs_sb = keep.tile([P, S // 16], U16, name="offs_sb")
@@ -42,7 +42,6 @@ def tile_picked_ynrtlg_lng_p_kernel(
         x1_sb = [keep.tile([P, 2, S], F32, name="x1_%d" % i) for i in range(2)]
         table_scales = keep.tile([P, T], U8, name="table_scales", align_bytes=64)
         table_words = [keep.tile([P, T], I32, name="table_words%d" % g, align_bytes=64) for g in range(PASSES)]
-        w3_raw = keep.tile([P, PACK, N], F32, name="w3_raw")
         unit_sb = keep.tile([P, PACK], F32, name="unit_sb")
         ident = keep.tile([P, P], F32, name="ident")
 
@@ -62,24 +61,24 @@ def tile_picked_ynrtlg_lng_p_kernel(
         nc.vector.memset(table_scales[:].bitcast(I32), 0)
         make_identity(nc, ident[:])
         nc.sync.dma_start(offs_sb[:], offs)
-        nc.sync.dma_start(out=x1_sb[0][:], in_=x1_dealt[:, 0:2, :])
         for q in range(4):
             nc.sync.dma_start(
                 out=table_scales[32 * q : 32 * q + 4 * PASSES, :].bitcast(I32),
                 in_=x_scales[:, 4 * q : 4 * q + 4, :].bitcast(I32),
             )
+        nc.sync.dma_start(out=x1_sb[0][:], in_=x1_dealt[:, 0:2, :])
         nc.sync.dma_start(out=x1_sb[1][:], in_=x1_dealt[:, 2:4, :])
         load_words(0)
         load_weight("w2_00", w2, 0, 0, HALF_H)
-        load_words(1)
         load_weight("w2_01", w2, 1, 0, HALF_H)
+        load_words(1)
         load_weight("w2_10", w2, 0, HALF_H, HALF_H)
         load_weight("w2_11", w2, 1, HALF_H, HALF_H)
         load_weight("w1_0", w1, 0, 0, H)
         load_weight("w1_1", w1, 1, 0, H)
         nc.sync.dma_start(out=unit_sb[:], in_=unit.rearrange("(p t) o -> p (t o)", t=PACK))
         nc.sync.dma_start(cmp_sb[:], cmp)
-        nc.sync.dma_start(out=w3_raw[:], in_=w3.rearrange("(p j) n -> p j n", j=PACK))
+        load_weight("w3", w3, 0, 0, N)
 
         def x1_rows(t):
             return x1_sb[t // 2][:, t % 2, :]
@@ -95,49 +94,59 @@ def tile_picked_ynrtlg_lng_p_kernel(
             return rows[:, 8 * pair : 8 * pair + 8, half * HALF_P : (half + 1) * HALF_P]
 
         logit = flipped_tile("logit")
-        logs = []
         for t in range(PACK):
-            bank = psum.tile([P, S], F32, name="bank_a", bufs=4)
+            bank = psum.tile([P, CHUNKS, P], F32, name="bank_a", bufs=2)
             for c in range(CHUNKS):
-                cols = slice(c * P, (c + 1) * P)
-                nc.tensor.transpose(bank[:, cols], x1_rows(t)[:, cols], ident[:])
-            ln1 = keep.tile([P, CHUNKS, P], F32, name="ln1_%d" % t)
-            ln2 = keep.tile([P, CHUNKS, P], F32, name="ln2_%d" % t)
-            view = bank[:].rearrange("s (c p) -> s c p", p=P)
-            nc.scalar.activation(out=ln1[:], in_=view, func=ACT.Ln, bias=TINY)
-            nc.scalar.activation(out=ln2[:], in_=view, func=ACT.Ln, scale=-1.0, bias=1.0)
-            logs.append((ln1, ln2))
+                nc.tensor.transpose(bank[:, c, :], x1_rows(t)[:, c * P : (c + 1) * P], ident[:])
+            ln1 = work.tile([P, CHUNKS, P], F32, name="ln1")
+            ln2 = work.tile([P, CHUNKS, P], F32, name="ln2")
+            nc.scalar.activation(out=ln1[:], in_=bank[:], func=ACT.Ln, bias=TINY)
+            nc.scalar.activation(out=ln2[:], in_=bank[:], func=ACT.Ln, scale=-1.0, bias=1.0)
+            nc.vector.tensor_tensor(out=by_slot(logit, t), in0=ln1[:], in1=ln2[:], op=ALU.subtract)
 
         picked_scales = keep.tile([P, S], U8, name="picked_scales", align_bytes=64)
         picked_words = [keep.tile([P, S], U32, name="picked_words%d" % g, align_bytes=64) for g in range(PASSES)]
 
-        def gather_words(g):
-            nc.vector.tensor_copy(picked_words[g][:], table_words[g][:].bitcast(U32).indirect(offs_sb[:]))
+        def gather_words(g, parts):
+            for i in range(parts):
+                first, last = i * S // parts, (i + 1) * S // parts
+                nc.vector.tensor_copy(
+                    picked_words[g][:, first:last],
+                    table_words[g][:].bitcast(U32).indirect(offs_sb[:, first // 16 : last // 16]),
+                )
 
         rounded = {}
         codes = {}
         scales = {}
 
-        def cast_weight(key, vector_m):
+        def cast_weight(key, vector_cols):
             width = raw[key].shape[2]
-            rounded[key] = keep.tile([P, PACK * width], BF16, name="bf_" + key, align_bytes=64)
-            src = raw[key][:].rearrange("p j (m t) -> p m t j", t=PACK)
-            dst = rounded[key][:].rearrange("p (t m j) -> p m t j", t=PACK, j=PACK)
-            count = width // PACK
-            if vector_m > 0:
-                nc.vector.tensor_copy(out=dst[:, 0:vector_m], in_=src[:, 0:vector_m])
-            for m in range(vector_m, count, CAST_STEP):
-                nc.scalar.copy(out=dst[:, m : m + CAST_STEP], in_=src[:, m : m + CAST_STEP])
+            rounded[key] = keep.tile([P, width, PACK], BF16, name="bf_" + key, align_bytes=64)
+
+            def weave(copy, first, last):
+                copy(
+                    out=rounded[key][:, first:last, :].rearrange("p (c i) j -> p c j i", i=4),
+                    in_=raw[key][:, :, first:last].rearrange("p j (c i) -> p c j i", i=4),
+                )
+
+            if vector_cols > 0:
+                weave(nc.vector.tensor_copy, 0, vector_cols)
+            for first in range(vector_cols, width, CAST_STEP):
+                weave(nc.scalar.copy, first, min(first + CAST_STEP, width))
 
         def quantize_weight(key):
             width = raw[key].shape[2]
             codes[key] = keep.tile([P, width], U32, name="codes_" + key, align_bytes=64)
             scales[key] = keep.tile([P, width], U8, name="scales_" + key, align_bytes=64)
-            nc.vector.quantize_mx(out=codes[key][:].bitcast(FP8X4), scales=scales[key][:], in_=rounded[key][:])
+            nc.vector.quantize_mx(
+                out=codes[key][:].bitcast(FP8X4),
+                scales=scales[key][:],
+                in_=rounded[key][:].rearrange("p h j -> p (h j)"),
+            )
 
-        def product(keys, hcols, chunks):
-            width = hcols.stop - hcols.start
-            bank = psum.tile([P, S], F32, name="bank_a", bufs=4)
+        def product(keys, chunks):
+            width = S // len(chunks)
+            bank = psum.tile([P, S], F32, name="bank_a", bufs=2)
             for i, c in enumerate(chunks):
                 cols = slice(c * P, (c + 1) * P)
                 for g in range(PASSES):
@@ -145,38 +154,22 @@ def tile_picked_ynrtlg_lng_p_kernel(
                         out=bank[:, i * width : (i + 1) * width],
                         lhsT=picked_words[g][:, cols].bitcast(FP8X4),
                         lhsT_scale=picked_scales[4 * g : P, cols],
-                        rhs=codes[keys[g]][:, hcols].bitcast(FP8X4),
-                        rhs_scale=scales[keys[g]][:, hcols],
+                        rhs=codes[keys[g]][:].bitcast(FP8X4),
+                        rhs_scale=scales[keys[g]][:],
                         start=(g == 0),
                         stop=(g == PASSES - 1),
                     )
             return bank
 
-        def local_terms(bounded, factor, odds, first, second):
-            run = odds.shape[2]
-            z = work.tile([P, S], F32, name="z")
-            nc.vector.scalar_tensor_tensor(
-                out=z[:].rearrange("s (a b) -> s a b", b=run),
-                in0=bounded[:].rearrange("s (a b) -> s a b", b=run),
-                scalar=ALPHA,
-                in1=odds,
-                op0=ALU.mult,
-                op1=ALU.add,
-            )
-            th = work.tile([P, S], F32, name="th")
+        def share(bounded, odds):
+            z = work.tile(odds.shape, F32, name="z")
+            nc.vector.scalar_tensor_tensor(out=z[:], in0=bounded, scalar=ALPHA, in1=odds, op0=ALU.mult, op1=ALU.add)
+            th = work.tile(odds.shape, F32, name="th")
             nc.scalar.activation(out=th[:], in_=z[:], func=ACT.Tanh, scale=-0.5)
-            th_view = th[:].rearrange("s (a b) -> s a b", b=run)
-            nc.vector.scalar_tensor_tensor(
-                out=first,
-                in0=th_view,
-                scalar=1.0,
-                in1=factor[:].rearrange("s (a b) -> s a b", b=run),
-                op0=ALU.add,
-                op1=ALU.mult,
-            )
-            nc.vector.scalar_tensor_tensor(
-                out=second, in0=th_view, scalar=1.0, in1=first, op0=ALU.add, op1=ALU.mult
-            )
+            return th
+
+        def times_share(dst, th, factor):
+            nc.vector.scalar_tensor_tensor(out=dst, in0=th[:], scalar=1.0, in1=factor, op0=ALU.add, op1=ALU.mult)
 
         def flip(bank, blocks, opens):
             for c in range(CHUNKS):
@@ -189,161 +182,174 @@ def tile_picked_ynrtlg_lng_p_kernel(
                     is_transpose=True,
                 )
 
-        nc.vector.tensor_copy(picked_scales[:], table_scales[:].indirect(offs_sb[:]))
-        gather_words(0)
-        cast_weight("w2_00", 64)
-        gather_words(1)
-        quantize_weight("w2_00")
-        cast_weight("w2_01", 64)
-        quantize_weight("w2_01")
-        for t in range(PACK):
-            nc.vector.tensor_tensor(out=by_slot(logit, t), in0=logs[t][0][:], in1=logs[t][1][:], op=ALU.subtract)
-
         first1 = flipped_tile("first1")
         second1 = flipped_tile("second1")
-
-        bounded1 = {}
+        tau1 = {}
 
         def start1(half, pair):
-            bank = product(["w2_%d%d" % (half, g) for g in range(PASSES)], slice(0, HALF_H), [2 * pair, 2 * pair + 1])
-            bounded1[half, pair] = work.tile([P, S], F32, name="bounded")
-            nc.scalar.activation(out=bounded1[half, pair][:], in_=bank[:], func=ACT.Tanh)
-
-        def terms1(half, pair):
-            tau1 = bounded1[half, pair]
-            local_terms(
-                tau1, tau1, by_half(logit, half, pair), by_half(first1, half, pair), by_half(second1, half, pair)
+            bank = product(["w2_%d%d" % (half, g) for g in range(PASSES)], [2 * pair, 2 * pair + 1])
+            tau1[half, pair] = work.tile([P, 2, PACK, HALF_P], F32, name="tau1")
+            nc.scalar.activation(
+                out=tau1[half, pair][:], in_=bank[:].rearrange("s (c p t) -> s c t p", c=2, t=PACK), func=ACT.Tanh
             )
 
-        start1(0, 0)
-        start1(0, 1)
-        cast_weight("w2_10", 64)
-        cast_weight("w2_11", 64)
-        quantize_weight("w2_10")
-        quantize_weight("w2_11")
-        cast_weight("w1_1", 64)
-        cast_weight("w1_0", 64)
-        quantize_weight("w1_0")
-        quantize_weight("w1_1")
-        terms1(0, 0)
-        start1(1, 0)
-        terms1(0, 1)
-        start1(1, 1)
-        terms1(1, 0)
-        terms1(1, 1)
+        def terms1(half, pair):
+            rows = tau1[half, pair][:].rearrange("s c t p -> s (c t) p")
+            th = share(rows, by_half(logit, half, pair))
+            times_share(by_half(first1, half, pair), th, rows)
+            times_share(by_half(second1, half, pair), th, by_half(first1, half, pair))
+
+        neg2 = flipped_tile("neg2")
+
+        def start2(c):
+            bank = product(["w1_0", "w1_1"], [c])
+            nc.scalar.activation(
+                out=neg2[:, c], in_=bank[:].rearrange("s (p t) -> s t p", t=PACK), func=ACT.Tanh, scale=-1.0
+            )
 
         unit_half = keep.tile([P, PACK], F32, name="unit_half")
         unit_quarter = keep.tile([P, PACK], F32, name="unit_quarter")
-        nc.gpsimd.tensor_scalar(unit_half[:], unit_sb[:], 0.5, 0.0, ALU.mult, ALU.add)
-        nc.gpsimd.tensor_scalar(unit_quarter[:], unit_sb[:], 0.25, 0.0, ALU.mult, ALU.add)
-
-        w3_bf = keep.tile([P, N, PACK], BF16, name="w3_bf", align_bytes=64)
-        w3_codes = keep.tile([P, N], U32, name="w3_codes", align_bytes=64)
-        w3_scales = keep.tile([P, N], U8, name="w3_scales", align_bytes=64)
         hid_rows = keep.tile([P, PACK, S], BF16, name="hid_rows")
 
         sums = {}
-        bounded2 = {}
+        th2 = {}
         gam2 = {}
+        first2 = {}
+        other = {}
 
-        def open_sums(t):
-            sums[t] = [psum.tile([P, S], F32, name="bank_b", bufs=4) for i in range(2)]
-            flip(sums[t][0], by_slot(first1, t), True)
-            flip(sums[t][1], by_slot(second1, t), True)
+        def open_first(t):
+            sums[t, 0] = psum.tile([P, S], F32, name="bank_b", bufs=6)
+            flip(sums[t, 0], by_slot(first1, t), True)
 
-        def start2(t):
-            bank = product(["w1_0", "w1_1"], slice(t * P, (t + 1) * P), range(CHUNKS))
-            bounded2[t] = work.tile([P, S], F32, name="bounded")
-            gam2[t] = work.tile([P, S], F32, name="gam2")
-            nc.scalar.activation(out=bounded2[t][:], in_=bank[:], func=ACT.Tanh, scale=-1.0)
-            nc.scalar.activation(out=gam2[t][:], in_=bounded2[t][:], func=ACT.Exp, scale=ALPHA)
+        def open_second(t):
+            sums[t, 1] = psum.tile([P, S], F32, name="bank_b", bufs=6)
+            flip(sums[t, 1], by_slot(second1, t), True)
 
-        def terms2(t):
-            first2 = work.tile([P, CHUNKS, P], F32, name="first2")
+        def share2(t):
+            gam2[t] = work.tile([P, CHUNKS, P], F32, name="gam2")
+            nc.scalar.activation(out=gam2[t][:], in_=by_slot(neg2, t), func=ACT.Exp, scale=ALPHA)
+            th2[t] = share(by_slot(neg2, t), by_slot(logit, t))
+
+        def close_first(t):
+            first2[t] = work.tile([P, CHUNKS, P], F32, name="first2")
+            times_share(first2[t][:], th2[t], gam2[t][:])
+            flip(sums[t, 0], first2[t][:], False)
+
+        def close_second(t):
             second2 = work.tile([P, CHUNKS, P], F32, name="second2")
-            local_terms(bounded2[t], gam2[t], by_slot(logit, t), first2[:], second2[:])
-            flip(sums[t][0], first2[:], False)
-            flip(sums[t][1], second2[:], False)
+            times_share(second2[:], th2[t], first2[t][:])
+            flip(sums[t, 1], second2[:], False)
 
-        def finish(t):
+        def excess(t, vector_halves):
             gex = work.tile([P, S], F32, name="gex")
             nc.vector.scalar_tensor_tensor(
-                out=gex[:], in0=sums[t][0][:], scalar=unit_half[:, t : t + 1], in1=x1_rows(t), op0=ALU.mult, op1=ALU.mult
+                out=gex[:], in0=sums[t, 0][:], scalar=unit_half[:, t : t + 1], in1=x1_rows(t), op0=ALU.mult, op1=ALU.mult
             )
-            other = work.tile([P, S], F32, name="other")
+            other[t] = work.tile([P, S], F32, name="other")
             for h in range(2):
                 cols = slice(h * HALF_S, (h + 1) * HALF_S)
                 named = gex[:].indirect(cmp_sb[:, h * HALF_S // 16 : (h + 1) * HALF_S // 16])
-                if t == PACK - 1 and h == 0:
-                    nc.vector.tensor_copy(other[:, cols], named)
+                if h < vector_halves:
+                    nc.vector.tensor_copy(other[t][:, cols], named)
                 else:
-                    nc.scalar.activation(out=other[:, cols], in_=named, func=ACT.Copy)
-            parts = 2 if t == PACK - 1 else 1
+                    nc.scalar.activation(out=other[t][:, cols], in_=named, func=ACT.Copy)
+
+        def hidden(t, parts):
             for h in range(parts):
                 cols = slice(h * S // parts, (h + 1) * S // parts)
                 nc.vector.scalar_tensor_tensor(
                     out=hid_rows[:, t, cols],
-                    in0=sums[t][1][:, cols],
+                    in0=sums[t, 1][:, cols],
                     scalar=unit_quarter[:, t : t + 1],
-                    in1=other[:, cols],
+                    in1=other[t][:, cols],
                     op0=ALU.mult,
                     op1=ALU.subtract,
                 )
 
-        def cast_w3():
-            nc.scalar.copy(
-                out=w3_bf[:].rearrange("p (c i) j -> p c j i", i=4),
-                in_=w3_raw[:].rearrange("p j (c i) -> p c j i", i=4),
-            )
-
-        def quantize_w3():
-            nc.vector.quantize_mx(
-                out=w3_codes[:].bitcast(FP8X4), scales=w3_scales[:], in_=w3_bf[:].rearrange("p n j -> p (n j)")
-            )
-
-        start2(0)
-        start2(1)
-        open_sums(0)
-        terms2(0)
-        start2(2)
-        open_sums(1)
-        terms2(1)
-        start2(3)
-        open_sums(2)
-        finish(0)
-        terms2(2)
-        cast_w3()
-        finish(1)
-        open_sums(3)
-        terms2(3)
-        quantize_w3()
-        finish(2)
-        finish(3)
-
-        for h in range(2):
-            hid_bf = work.tile([P, HALF_S, PACK], BF16, name="hid_bf", align_bytes=64)
-            weave = nc.vector.tensor_copy if h == 0 else nc.scalar.copy
+        def last_product(first, last, weave):
+            width = last - first
+            hid_bf = work.tile([P, width, PACK], BF16, name="hid_bf", align_bytes=64)
             weave(
                 out=hid_bf[:].rearrange("p (c i) t -> p c t i", i=4),
-                in_=hid_rows[:, :, h * HALF_S : (h + 1) * HALF_S].rearrange("p t (c i) -> p c t i", i=4),
+                in_=hid_rows[:, :, first:last].rearrange("p t (c i) -> p c t i", i=4),
             )
-            hid_codes = work.tile([P, HALF_S], U32, name="hid_codes", align_bytes=64)
-            hid_scales = work.tile([P, HALF_S], U8, name="hid_scales", align_bytes=64)
+            hid_codes = work.tile([P, width], U32, name="hid_codes", align_bytes=64)
+            hid_scales = work.tile([P, width], U8, name="hid_scales", align_bytes=64)
             nc.vector.quantize_mx(
-                out=hid_codes[:].bitcast(FP8X4),
-                scales=hid_scales[:],
-                in_=hid_bf[:].rearrange("p s t -> p (s t)"),
+                out=hid_codes[:].bitcast(FP8X4), scales=hid_scales[:], in_=hid_bf[:].rearrange("p s t -> p (s t)")
             )
-            bank = psum.tile([P, HALF_S], F32, name="bank_a", bufs=4)
+            bank = psum.tile([P, width], F32, name="bank_a", bufs=2)
             nc.tensor.matmul_mx(
                 out=bank[:],
-                lhsT=w3_codes[:].bitcast(FP8X4),
-                lhsT_scale=w3_scales[:],
+                lhsT=codes["w3"][:].bitcast(FP8X4),
+                lhsT_scale=scales["w3"][:],
                 rhs=hid_codes[:].bitcast(FP8X4),
                 rhs_scale=hid_scales[:],
                 start=True,
                 stop=True,
             )
-            result = work.tile([P, HALF_S], F32, name="result")
+            result = work.tile([P, width], F32, name="result")
             nc.scalar.copy(out=result[:], in_=bank[:])
-            nc.sync.dma_start(out=out[:, h * HALF_S : (h + 1) * HALF_S], in_=result[:])
+            nc.sync.dma_start(out=out[:, first:last], in_=result[:])
+
+        nc.vector.tensor_copy(picked_scales[:], table_scales[:].indirect(offs_sb[:]))
+        nc.gpsimd.tensor_scalar(unit_half[:], unit_sb[:], 0.5, 0.0, ALU.mult, ALU.add)
+        nc.gpsimd.tensor_scalar(unit_quarter[:], unit_sb[:], 0.25, 0.0, ALU.mult, ALU.add)
+        gather_words(0, 1)
+        cast_weight("w2_00", HALF_H)
+        cast_weight("w2_01", HALF_H)
+        quantize_weight("w2_00")
+        quantize_weight("w2_01")
+        gather_words(1, 2)
+        start1(0, 0)
+        start1(0, 1)
+        cast_weight("w2_10", HALF_H)
+        cast_weight("w2_11", HALF_H)
+        quantize_weight("w2_10")
+        quantize_weight("w2_11")
+        start1(1, 0)
+        start1(1, 1)
+        cast_weight("w1_1", 256)
+        cast_weight("w1_0", 256)
+        quantize_weight("w1_0")
+        quantize_weight("w1_1")
+        start2(0)
+        start2(1)
+        start2(2)
+        start2(3)
+        terms1(0, 0)
+        terms1(0, 1)
+        terms1(1, 0)
+        terms1(1, 1)
+        share2(0)
+        share2(1)
+        open_first(0)
+        close_first(0)
+        share2(2)
+        open_first(1)
+        close_first(1)
+        excess(0, 0)
+        share2(3)
+        open_first(2)
+        close_first(2)
+        excess(1, 0)
+        open_first(3)
+        close_first(3)
+        excess(2, 0)
+        excess(3, 0)
+        cast_weight("w3", 0)
+        quantize_weight("w3")
+        open_second(0)
+        close_second(0)
+        open_second(1)
+        close_second(1)
+        hidden(0, 1)
+        open_second(2)
+        close_second(2)
+        hidden(1, 1)
+        open_second(3)
+        close_second(3)
+        hidden(2, 1)
+        hidden(3, 2)
+        last_product(0, HALF_S, nc.vector.tensor_copy)
+        last_product(HALF_S, S, nc.scalar.copy)

@@ -95,11 +95,11 @@ def tile_picked_ynrtlg_lng_p_kernel(
 
         logit = flipped_tile("logit")
         for t in range(PACK):
-            bank = psum.tile([P, CHUNKS, P], F32, name="bank_a", bufs=2)
+            bank = psum.tile([P, CHUNKS, P], F32, name="bank_a", bufs=4)
             for c in range(CHUNKS):
                 nc.tensor.transpose(bank[:, c, :], x1_rows(t)[:, c * P : (c + 1) * P], ident[:])
-            ln1 = work.tile([P, CHUNKS, P], F32, name="ln1")
-            ln2 = work.tile([P, CHUNKS, P], F32, name="ln2")
+            ln1 = work.tile([P, CHUNKS, P], F32, name="ln1", bufs=3)
+            ln2 = work.tile([P, CHUNKS, P], F32, name="ln2", bufs=3)
             nc.scalar.activation(out=ln1[:], in_=bank[:], func=ACT.Ln, bias=TINY)
             nc.scalar.activation(out=ln2[:], in_=bank[:], func=ACT.Ln, scale=-1.0, bias=1.0)
             nc.vector.tensor_tensor(out=by_slot(logit, t), in0=ln1[:], in1=ln2[:], op=ALU.subtract)
@@ -146,25 +146,25 @@ def tile_picked_ynrtlg_lng_p_kernel(
 
         def product(keys, chunks):
             width = S // len(chunks)
-            bank = psum.tile([P, S], F32, name="bank_a", bufs=2)
-            for i, c in enumerate(chunks):
-                cols = slice(c * P, (c + 1) * P)
-                for g in range(PASSES):
+            bank = psum.tile([P, S], F32, name="bank_a", bufs=4)
+            for g in range(PASSES):
+                for i, c in enumerate(chunks):
+                    cols = slice(c * P, (c + 1) * P)
                     nc.tensor.matmul_mx(
                         out=bank[:, i * width : (i + 1) * width],
                         lhsT=picked_words[g][:, cols].bitcast(FP8X4),
                         lhsT_scale=picked_scales[4 * g : P, cols],
                         rhs=codes[keys[g]][:].bitcast(FP8X4),
                         rhs_scale=scales[keys[g]][:],
-                        start=(g == 0),
-                        stop=(g == PASSES - 1),
+                        start=(g == 0 and i == 0),
+                        stop=(g == PASSES - 1 and i == len(chunks) - 1),
                     )
             return bank
 
-        def share(bounded, odds):
+        def share(bounded, odds, tag):
             z = work.tile(odds.shape, F32, name="z")
             nc.vector.scalar_tensor_tensor(out=z[:], in0=bounded, scalar=ALPHA, in1=odds, op0=ALU.mult, op1=ALU.add)
-            th = work.tile(odds.shape, F32, name="th")
+            th = work.tile(odds.shape, F32, name=tag)
             nc.scalar.activation(out=th[:], in_=z[:], func=ACT.Tanh, scale=-0.5)
             return th
 
@@ -195,16 +195,31 @@ def tile_picked_ynrtlg_lng_p_kernel(
 
         def terms1(half, pair):
             rows = tau1[half, pair][:].rearrange("s c t p -> s (c t) p")
-            th = share(rows, by_half(logit, half, pair))
+            th = share(rows, by_half(logit, half, pair), "th1")
             times_share(by_half(first1, half, pair), th, rows)
             times_share(by_half(second1, half, pair), th, by_half(first1, half, pair))
 
         neg2 = flipped_tile("neg2")
 
+        banks2 = {}
+
+        def product2(c, g):
+            if g == 0:
+                banks2[c] = psum.tile([P, S], F32, name="bank_a", bufs=4)
+            cols = slice(c * P, (c + 1) * P)
+            nc.tensor.matmul_mx(
+                out=banks2[c][:],
+                lhsT=picked_words[g][:, cols].bitcast(FP8X4),
+                lhsT_scale=picked_scales[4 * g : P, cols],
+                rhs=codes["w1_%d" % g][:].bitcast(FP8X4),
+                rhs_scale=scales["w1_%d" % g][:],
+                start=(g == 0),
+                stop=(g == PASSES - 1),
+            )
+
         def start2(c):
-            bank = product(["w1_0", "w1_1"], [c])
             nc.scalar.activation(
-                out=neg2[:, c], in_=bank[:].rearrange("s (p t) -> s t p", t=PACK), func=ACT.Tanh, scale=-1.0
+                out=neg2[:, c], in_=banks2[c][:].rearrange("s (p t) -> s t p", t=PACK), func=ACT.Tanh, scale=-1.0
             )
 
         unit_half = keep.tile([P, PACK], F32, name="unit_half")
@@ -218,17 +233,17 @@ def tile_picked_ynrtlg_lng_p_kernel(
         other = {}
 
         def open_first(t):
-            sums[t, 0] = psum.tile([P, S], F32, name="bank_b", bufs=6)
+            sums[t, 0] = psum.tile([P, S], F32, name="bank_b", bufs=4)
             flip(sums[t, 0], by_slot(first1, t), True)
 
         def open_second(t):
-            sums[t, 1] = psum.tile([P, S], F32, name="bank_b", bufs=6)
+            sums[t, 1] = psum.tile([P, S], F32, name="bank_a", bufs=4)
             flip(sums[t, 1], by_slot(second1, t), True)
 
         def share2(t):
             gam2[t] = work.tile([P, CHUNKS, P], F32, name="gam2")
             nc.scalar.activation(out=gam2[t][:], in_=by_slot(neg2, t), func=ACT.Exp, scale=ALPHA)
-            th2[t] = share(by_slot(neg2, t), by_slot(logit, t))
+            th2[t] = share(by_slot(neg2, t), by_slot(logit, t), "th2")
 
         def close_first(t):
             first2[t] = work.tile([P, CHUNKS, P], F32, name="first2")
@@ -254,19 +269,17 @@ def tile_picked_ynrtlg_lng_p_kernel(
                 else:
                     nc.scalar.activation(out=other[t][:, cols], in_=named, func=ACT.Copy)
 
-        def hidden(t, parts):
-            for h in range(parts):
-                cols = slice(h * S // parts, (h + 1) * S // parts)
-                nc.vector.scalar_tensor_tensor(
-                    out=hid_rows[:, t, cols],
-                    in0=sums[t, 1][:, cols],
-                    scalar=unit_quarter[:, t : t + 1],
-                    in1=other[t][:, cols],
-                    op0=ALU.mult,
-                    op1=ALU.subtract,
-                )
+        def hidden(t, first, last):
+            nc.vector.scalar_tensor_tensor(
+                out=hid_rows[:, t, first:last],
+                in0=sums[t, 1][:, first:last],
+                scalar=unit_quarter[:, t : t + 1],
+                in1=other[t][:, first:last],
+                op0=ALU.mult,
+                op1=ALU.subtract,
+            )
 
-        def last_product(first, last, weave):
+        def last_product(first, last, weave, empty):
             width = last - first
             hid_bf = work.tile([P, width, PACK], BF16, name="hid_bf", align_bytes=64)
             weave(
@@ -278,7 +291,7 @@ def tile_picked_ynrtlg_lng_p_kernel(
             nc.vector.quantize_mx(
                 out=hid_codes[:].bitcast(FP8X4), scales=hid_scales[:], in_=hid_bf[:].rearrange("p s t -> p (s t)")
             )
-            bank = psum.tile([P, width], F32, name="bank_a", bufs=2)
+            bank = psum.tile([P, width], F32, name="bank_b", bufs=4)
             nc.tensor.matmul_mx(
                 out=bank[:],
                 lhsT=codes["w3"][:].bitcast(FP8X4),
@@ -289,38 +302,46 @@ def tile_picked_ynrtlg_lng_p_kernel(
                 stop=True,
             )
             result = work.tile([P, width], F32, name="result")
-            nc.scalar.copy(out=result[:], in_=bank[:])
+            empty(out=result[:], in_=bank[:])
             nc.sync.dma_start(out=out[:, first:last], in_=result[:])
 
         nc.vector.tensor_copy(picked_scales[:], table_scales[:].indirect(offs_sb[:]))
         nc.gpsimd.tensor_scalar(unit_half[:], unit_sb[:], 0.5, 0.0, ALU.mult, ALU.add)
         nc.gpsimd.tensor_scalar(unit_quarter[:], unit_sb[:], 0.25, 0.0, ALU.mult, ALU.add)
         gather_words(0, 1)
-        cast_weight("w2_00", HALF_H)
+        cast_weight("w2_00", 0)
         cast_weight("w2_01", HALF_H)
         quantize_weight("w2_00")
         quantize_weight("w2_01")
         gather_words(1, 2)
-        start1(0, 0)
-        start1(0, 1)
-        cast_weight("w2_10", HALF_H)
-        cast_weight("w2_11", HALF_H)
+        cast_weight("w2_10", 256)
+        cast_weight("w2_11", 256)
         quantize_weight("w2_10")
         quantize_weight("w2_11")
+        cast_weight("w1_0", 192)
+        quantize_weight("w1_0")
+        cast_weight("w1_1", 256)
+        quantize_weight("w1_1")
+        start1(0, 0)
+        start1(0, 1)
         start1(1, 0)
         start1(1, 1)
-        cast_weight("w1_1", 256)
-        cast_weight("w1_0", 256)
-        quantize_weight("w1_0")
-        quantize_weight("w1_1")
-        start2(0)
-        start2(1)
-        start2(2)
-        start2(3)
+        product2(0, 0)
+        product2(1, 0)
+        product2(2, 0)
+        product2(3, 0)
+        product2(0, 1)
+        product2(1, 1)
+        product2(2, 1)
+        product2(3, 1)
         terms1(0, 0)
         terms1(0, 1)
         terms1(1, 0)
         terms1(1, 1)
+        start2(0)
+        start2(1)
+        start2(2)
+        start2(3)
         share2(0)
         share2(1)
         open_first(0)
@@ -337,19 +358,24 @@ def tile_picked_ynrtlg_lng_p_kernel(
         close_first(3)
         excess(2, 0)
         excess(3, 0)
-        cast_weight("w3", 0)
-        quantize_weight("w3")
         open_second(0)
         close_second(0)
         open_second(1)
         close_second(1)
-        hidden(0, 1)
         open_second(2)
         close_second(2)
-        hidden(1, 1)
         open_second(3)
         close_second(3)
-        hidden(2, 1)
-        hidden(3, 2)
-        last_product(0, HALF_S, nc.vector.tensor_copy)
-        last_product(HALF_S, S, nc.scalar.copy)
+        cast_weight("w3", 0)
+        quantize_weight("w3")
+        hidden(0, 0, 256)
+        hidden(1, 0, 256)
+        hidden(2, 0, 256)
+        hidden(3, 0, 256)
+        hidden(0, 256, S)
+        hidden(1, 256, S)
+        hidden(2, 256, S)
+        hidden(3, 256, S)
+        last_product(0, 256, nc.scalar.copy, nc.scalar.copy)
+        last_product(256, 384, nc.scalar.copy, nc.scalar.copy)
+        last_product(384, S, nc.vector.tensor_copy, nc.vector.tensor_copy)

@@ -20,12 +20,19 @@ P = 128
 PACK = 4
 PASSES = K // (P * PACK)
 CHUNKS = S // P
-ALPHA = 0.7
-TINY = 2.0 ** -60
+QUADRANTS = 4
+SCALE_ROWS = 4
+LIST_ROWS = 16
 HALF_S = S // 2
 HALF_H = H // 2
 HALF_P = P // 2
-CAST_STEP = 128
+LINE = 4
+BANKS = 4
+ALPHA = 0.7
+TINY = 2.0 ** -60
+
+W1_VECTOR_COLUMNS = (192, 256)
+SCALAR_COPY_COLUMNS = 128
 
 
 def tile_picked_ynrtlg_lng_p_kernel(
@@ -35,16 +42,15 @@ def tile_picked_ynrtlg_lng_p_kernel(
     with ExitStack() as ctx:
         keep = ctx.enter_context(tc.tile_pool(name="keep", bufs=1))
         work = ctx.enter_context(tc.tile_pool(name="work", bufs=4))
-        psum = ctx.enter_context(tc.psum_pool(name="psum", bufs=4))
+        psum = ctx.enter_context(tc.psum_pool(name="psum", bufs=BANKS))
 
-        offs_sb = keep.tile([P, S // 16], U16, name="offs_sb")
-        cmp_sb = keep.tile([P, S // 16], U16, name="cmp_sb")
+        offs_sb = keep.tile([P, S // LIST_ROWS], U16, name="offs_sb")
+        cmp_sb = keep.tile([P, S // LIST_ROWS], U16, name="cmp_sb")
         x1_sb = [keep.tile([P, 2, S], F32, name="x1_%d" % i) for i in range(2)]
         table_scales = keep.tile([P, T], U8, name="table_scales", align_bytes=64)
         table_words = [keep.tile([P, T], I32, name="table_words%d" % g, align_bytes=64) for g in range(PASSES)]
         unit_sb = keep.tile([P, PACK], F32, name="unit_sb")
         ident = keep.tile([P, P], F32, name="ident")
-
         raw = {}
 
         def load_weight(key, w, g, first, width):
@@ -53,86 +59,82 @@ def tile_picked_ynrtlg_lng_p_kernel(
             nc.sync.dma_start(out=raw[key][:], in_=rows.rearrange("(p j) h -> p j h", j=PACK))
 
         def load_words(g):
-            nc.sync.dma_start(
-                out=table_words[g][:], in_=x_words[g].rearrange("p n t -> p (n t)").bitcast(I32)
-            )
+            nc.sync.dma_start(out=table_words[g][:], in_=x_words[g].rearrange("p n t -> p (n t)").bitcast(I32))
 
-        x1_dealt = x1.rearrange("(p t) s -> p t s", t=PACK)
         nc.vector.memset(table_scales[:].bitcast(I32), 0)
         make_identity(nc, ident[:])
         nc.sync.dma_start(offs_sb[:], offs)
-        for q in range(4):
+        for q in range(QUADRANTS):
             nc.sync.dma_start(
-                out=table_scales[32 * q : 32 * q + 4 * PASSES, :].bitcast(I32),
-                in_=x_scales[:, 4 * q : 4 * q + 4, :].bitcast(I32),
+                out=table_scales[32 * q : 32 * q + SCALE_ROWS * PASSES, :].bitcast(I32),
+                in_=x_scales[:, SCALE_ROWS * q : SCALE_ROWS * (q + 1), :].bitcast(I32),
             )
-        nc.sync.dma_start(out=x1_sb[0][:], in_=x1_dealt[:, 0:2, :])
-        nc.sync.dma_start(out=x1_sb[1][:], in_=x1_dealt[:, 2:4, :])
-        load_words(0)
-        load_weight("w2_00", w2, 0, 0, HALF_H)
-        load_weight("w2_01", w2, 1, 0, HALF_H)
-        load_words(1)
-        load_weight("w2_10", w2, 0, HALF_H, HALF_H)
-        load_weight("w2_11", w2, 1, HALF_H, HALF_H)
-        load_weight("w1_0", w1, 0, 0, H)
-        load_weight("w1_1", w1, 1, 0, H)
+        x1_dealt = x1.rearrange("(p t) s -> p t s", t=PACK)
+        for i in range(2):
+            nc.sync.dma_start(out=x1_sb[i][:], in_=x1_dealt[:, 2 * i : 2 * i + 2, :])
         nc.sync.dma_start(out=unit_sb[:], in_=unit.rearrange("(p t) o -> p (t o)", t=PACK))
+        load_words(0)
+        for g in range(PASSES):
+            load_weight("w2_0%d" % g, w2, g, 0, HALF_H)
+        load_words(1)
+        for g in range(PASSES):
+            load_weight("w2_1%d" % g, w2, g, HALF_H, HALF_H)
+        for g in range(PASSES):
+            load_weight("w1_%d" % g, w1, g, 0, H)
         nc.sync.dma_start(cmp_sb[:], cmp)
         load_weight("w3", w3, 0, 0, N)
 
         def x1_rows(t):
             return x1_sb[t // 2][:, t % 2, :]
 
-        def flipped_tile(name):
+        def turned_tile(name):
             return keep.tile([P, CHUNKS, PACK, P], F32, name=name)
 
         def by_slot(tile, t):
             return tile[:, :, t, :]
 
-        def by_half(tile, half, pair):
-            rows = tile[:].rearrange("s c t p -> s (c t) p")
-            return rows[:, 8 * pair : 8 * pair + 8, half * HALF_P : (half + 1) * HALF_P]
+        def by_piece(tile, half, pair):
+            runs = tile[:].rearrange("r c t p -> r (c t) p")
+            return runs[:, 2 * PACK * pair : 2 * PACK * (pair + 1), half * HALF_P : (half + 1) * HALF_P]
 
-        logit = flipped_tile("logit")
+        odds = turned_tile("odds")
         for t in range(PACK):
-            bank = psum.tile([P, CHUNKS, P], F32, name="bank_a", bufs=4)
+            bank = psum.tile([P, CHUNKS, P], F32, name="bank_a")
             for c in range(CHUNKS):
                 nc.tensor.transpose(bank[:, c, :], x1_rows(t)[:, c * P : (c + 1) * P], ident[:])
             ln1 = work.tile([P, CHUNKS, P], F32, name="ln1", bufs=3)
             ln2 = work.tile([P, CHUNKS, P], F32, name="ln2", bufs=3)
             nc.scalar.activation(out=ln1[:], in_=bank[:], func=ACT.Ln, bias=TINY)
             nc.scalar.activation(out=ln2[:], in_=bank[:], func=ACT.Ln, scale=-1.0, bias=1.0)
-            nc.vector.tensor_tensor(out=by_slot(logit, t), in0=ln1[:], in1=ln2[:], op=ALU.subtract)
+            nc.vector.tensor_tensor(out=by_slot(odds, t), in0=ln1[:], in1=ln2[:], op=ALU.subtract)
 
         picked_scales = keep.tile([P, S], U8, name="picked_scales", align_bytes=64)
         picked_words = [keep.tile([P, S], U32, name="picked_words%d" % g, align_bytes=64) for g in range(PASSES)]
 
-        def gather_words(g, parts):
-            for i in range(parts):
-                first, last = i * S // parts, (i + 1) * S // parts
-                nc.vector.tensor_copy(
-                    picked_words[g][:, first:last],
-                    table_words[g][:].bitcast(U32).indirect(offs_sb[:, first // 16 : last // 16]),
-                )
+        def gather_words(g, first, last):
+            nc.vector.tensor_copy(
+                picked_words[g][:, first:last],
+                table_words[g][:].bitcast(U32).indirect(offs_sb[:, first // LIST_ROWS : last // LIST_ROWS]),
+            )
+
+        def weave(copy, woven, rows):
+            copy(
+                out=woven.rearrange("p (m i) j -> p m j i", i=LINE),
+                in_=rows.rearrange("p j (m i) -> p m j i", i=LINE),
+            )
 
         rounded = {}
         codes = {}
         scales = {}
 
-        def cast_weight(key, vector_cols):
+        def round_weight(key, vector_columns):
             width = raw[key].shape[2]
             rounded[key] = keep.tile([P, width, PACK], BF16, name="bf_" + key, align_bytes=64)
-
-            def weave(copy, first, last):
-                copy(
-                    out=rounded[key][:, first:last, :].rearrange("p (c i) j -> p c j i", i=4),
-                    in_=raw[key][:, :, first:last].rearrange("p j (c i) -> p c j i", i=4),
-                )
-
-            if vector_cols > 0:
-                weave(nc.vector.tensor_copy, 0, vector_cols)
-            for first in range(vector_cols, width, CAST_STEP):
-                weave(nc.scalar.copy, first, min(first + CAST_STEP, width))
+            shares = [(nc.vector.tensor_copy, 0, vector_columns)] if vector_columns > 0 else []
+            for first in range(vector_columns, width, SCALAR_COPY_COLUMNS):
+                shares.append((nc.scalar.copy, first, min(first + SCALAR_COPY_COLUMNS, width)))
+            for copy, first, last in shares:
+                weave(copy, rounded[key][:, first:last, :], raw[key][:, :, first:last])
 
         def quantize_weight(key):
             width = raw[key].shape[2]
@@ -144,34 +146,31 @@ def tile_picked_ynrtlg_lng_p_kernel(
                 in_=rounded[key][:].rearrange("p h j -> p (h j)"),
             )
 
-        def product(keys, chunks):
-            width = S // len(chunks)
-            bank = psum.tile([P, S], F32, name="bank_a", bufs=4)
-            for g in range(PASSES):
-                for i, c in enumerate(chunks):
-                    cols = slice(c * P, (c + 1) * P)
-                    nc.tensor.matmul_mx(
-                        out=bank[:, i * width : (i + 1) * width],
-                        lhsT=picked_words[g][:, cols].bitcast(FP8X4),
-                        lhsT_scale=picked_scales[4 * g : P, cols],
-                        rhs=codes[keys[g]][:].bitcast(FP8X4),
-                        rhs_scale=scales[keys[g]][:],
-                        start=(g == 0 and i == 0),
-                        stop=(g == PASSES - 1 and i == len(chunks) - 1),
-                    )
-            return bank
+        def picked_product(dst, c, g, key, start, stop):
+            cols = slice(c * P, (c + 1) * P)
+            nc.tensor.matmul_mx(
+                out=dst,
+                lhsT=picked_words[g][:, cols].bitcast(FP8X4),
+                lhsT_scale=picked_scales[SCALE_ROWS * g : P, cols],
+                rhs=codes[key][:].bitcast(FP8X4),
+                rhs_scale=scales[key][:],
+                start=start,
+                stop=stop,
+            )
 
-        def share(bounded, odds, tag):
-            z = work.tile(odds.shape, F32, name="z")
-            nc.vector.scalar_tensor_tensor(out=z[:], in0=bounded, scalar=ALPHA, in1=odds, op0=ALU.mult, op1=ALU.add)
-            th = work.tile(odds.shape, F32, name=tag)
-            nc.scalar.activation(out=th[:], in_=z[:], func=ACT.Tanh, scale=-0.5)
-            return th
+        def composition(bounded, piece_odds, tag):
+            z = work.tile(piece_odds.shape, F32, name="z")
+            nc.vector.scalar_tensor_tensor(
+                out=z[:], in0=bounded, scalar=ALPHA, in1=piece_odds, op0=ALU.mult, op1=ALU.add
+            )
+            centred = work.tile(piece_odds.shape, F32, name=tag)
+            nc.scalar.activation(out=centred[:], in_=z[:], func=ACT.Tanh, scale=-0.5)
+            return centred
 
-        def times_share(dst, th, factor):
-            nc.vector.scalar_tensor_tensor(out=dst, in0=th[:], scalar=1.0, in1=factor, op0=ALU.add, op1=ALU.mult)
+        def times_twice_a(dst, centred, factor):
+            nc.vector.scalar_tensor_tensor(out=dst, in0=centred[:], scalar=1.0, in1=factor, op0=ALU.add, op1=ALU.mult)
 
-        def flip(bank, blocks, opens):
+        def turn_back(bank, blocks, opens):
             for c in range(CHUNKS):
                 nc.tensor.matmul(
                     bank[:, c * P : (c + 1) * P],
@@ -182,116 +181,116 @@ def tile_picked_ynrtlg_lng_p_kernel(
                     is_transpose=True,
                 )
 
-        first1 = flipped_tile("first1")
-        second1 = flipped_tile("second1")
+        single1 = turned_tile("single1")
+        double1 = turned_tile("double1")
         tau1 = {}
 
-        def start1(half, pair):
-            bank = product(["w2_%d%d" % (half, g) for g in range(PASSES)], [2 * pair, 2 * pair + 1])
+        def bound1(half, pair):
+            bank = psum.tile([P, S], F32, name="bank_a")
+            for g in range(PASSES):
+                for i in range(2):
+                    picked_product(
+                        bank[:, i * HALF_H : (i + 1) * HALF_H],
+                        2 * pair + i,
+                        g,
+                        "w2_%d%d" % (half, g),
+                        start=(g == 0 and i == 0),
+                        stop=(g == PASSES - 1 and i == 1),
+                    )
             tau1[half, pair] = work.tile([P, 2, PACK, HALF_P], F32, name="tau1")
             nc.scalar.activation(
-                out=tau1[half, pair][:], in_=bank[:].rearrange("s (c p t) -> s c t p", c=2, t=PACK), func=ACT.Tanh
+                out=tau1[half, pair][:], in_=bank[:].rearrange("r (c p t) -> r c t p", c=2, t=PACK), func=ACT.Tanh
             )
 
         def terms1(half, pair):
-            rows = tau1[half, pair][:].rearrange("s c t p -> s (c t) p")
-            th = share(rows, by_half(logit, half, pair), "th1")
-            times_share(by_half(first1, half, pair), th, rows)
-            times_share(by_half(second1, half, pair), th, by_half(first1, half, pair))
+            factor = tau1[half, pair][:].rearrange("r c t p -> r (c t) p")
+            centred = composition(factor, by_piece(odds, half, pair), "centred1")
+            times_twice_a(by_piece(single1, half, pair), centred, factor)
+            times_twice_a(by_piece(double1, half, pair), centred, by_piece(single1, half, pair))
 
-        neg2 = flipped_tile("neg2")
-
+        minus_tanh2 = turned_tile("minus_tanh2")
         banks2 = {}
 
         def product2(c, g):
             if g == 0:
-                banks2[c] = psum.tile([P, S], F32, name="bank_a", bufs=4)
-            cols = slice(c * P, (c + 1) * P)
-            nc.tensor.matmul_mx(
-                out=banks2[c][:],
-                lhsT=picked_words[g][:, cols].bitcast(FP8X4),
-                lhsT_scale=picked_scales[4 * g : P, cols],
-                rhs=codes["w1_%d" % g][:].bitcast(FP8X4),
-                rhs_scale=scales["w1_%d" % g][:],
-                start=(g == 0),
-                stop=(g == PASSES - 1),
-            )
+                banks2[c] = psum.tile([P, H], F32, name="bank_a")
+            picked_product(banks2[c][:], c, g, "w1_%d" % g, start=(g == 0), stop=(g == PASSES - 1))
 
-        def start2(c):
+        def bound2(c):
             nc.scalar.activation(
-                out=neg2[:, c], in_=banks2[c][:].rearrange("s (p t) -> s t p", t=PACK), func=ACT.Tanh, scale=-1.0
+                out=minus_tanh2[:, c],
+                in_=banks2[c][:].rearrange("r (p t) -> r t p", t=PACK),
+                func=ACT.Tanh,
+                scale=-1.0,
             )
 
         unit_half = keep.tile([P, PACK], F32, name="unit_half")
         unit_quarter = keep.tile([P, PACK], F32, name="unit_quarter")
         hid_rows = keep.tile([P, PACK, S], BF16, name="hid_rows")
-
-        sums = {}
-        th2 = {}
+        centred2 = {}
         gam2 = {}
-        first2 = {}
-        other = {}
+        single2 = {}
+        singles = {}
+        doubles = {}
+        named = {}
 
-        def open_first(t):
-            sums[t, 0] = psum.tile([P, S], F32, name="bank_b", bufs=4)
-            flip(sums[t, 0], by_slot(first1, t), True)
-
-        def open_second(t):
-            sums[t, 1] = psum.tile([P, S], F32, name="bank_a", bufs=4)
-            flip(sums[t, 1], by_slot(second1, t), True)
-
-        def share2(t):
+        def composition2(t):
             gam2[t] = work.tile([P, CHUNKS, P], F32, name="gam2")
-            nc.scalar.activation(out=gam2[t][:], in_=by_slot(neg2, t), func=ACT.Exp, scale=ALPHA)
-            th2[t] = share(by_slot(neg2, t), by_slot(logit, t), "th2")
+            nc.scalar.activation(out=gam2[t][:], in_=by_slot(minus_tanh2, t), func=ACT.Exp, scale=ALPHA)
+            centred2[t] = composition(by_slot(minus_tanh2, t), by_slot(odds, t), "centred2")
 
-        def close_first(t):
-            first2[t] = work.tile([P, CHUNKS, P], F32, name="first2")
-            times_share(first2[t][:], th2[t], gam2[t][:])
-            flip(sums[t, 0], first2[t][:], False)
+        def sum_singles(t):
+            singles[t] = psum.tile([P, S], F32, name="bank_b")
+            turn_back(singles[t], by_slot(single1, t), True)
+            single2[t] = work.tile([P, CHUNKS, P], F32, name="single2")
+            times_twice_a(single2[t][:], centred2[t], gam2[t][:])
+            turn_back(singles[t], single2[t][:], False)
 
-        def close_second(t):
-            second2 = work.tile([P, CHUNKS, P], F32, name="second2")
-            times_share(second2[:], th2[t], first2[t][:])
-            flip(sums[t, 1], second2[:], False)
+        def sum_doubles(t):
+            doubles[t] = psum.tile([P, S], F32, name="bank_a")
+            turn_back(doubles[t], by_slot(double1, t), True)
+            double2 = work.tile([P, CHUNKS, P], F32, name="double2")
+            times_twice_a(double2[:], centred2[t], single2[t][:])
+            turn_back(doubles[t], double2[:], False)
 
-        def excess(t, vector_halves):
-            gex = work.tile([P, S], F32, name="gex")
+        def look_up_excess(t):
+            excess = work.tile([P, S], F32, name="excess")
             nc.vector.scalar_tensor_tensor(
-                out=gex[:], in0=sums[t, 0][:], scalar=unit_half[:, t : t + 1], in1=x1_rows(t), op0=ALU.mult, op1=ALU.mult
+                out=excess[:],
+                in0=singles[t][:],
+                scalar=unit_half[:, t : t + 1],
+                in1=x1_rows(t),
+                op0=ALU.mult,
+                op1=ALU.mult,
             )
-            other[t] = work.tile([P, S], F32, name="other")
-            for h in range(2):
-                cols = slice(h * HALF_S, (h + 1) * HALF_S)
-                named = gex[:].indirect(cmp_sb[:, h * HALF_S // 16 : (h + 1) * HALF_S // 16])
-                if h < vector_halves:
-                    nc.vector.tensor_copy(other[t][:, cols], named)
-                else:
-                    nc.scalar.activation(out=other[t][:, cols], in_=named, func=ACT.Copy)
+            named[t] = work.tile([P, S], F32, name="named")
+            for first in (0, HALF_S):
+                nc.scalar.activation(
+                    out=named[t][:, first : first + HALF_S],
+                    in_=excess[:].indirect(cmp_sb[:, first // LIST_ROWS : (first + HALF_S) // LIST_ROWS]),
+                    func=ACT.Copy,
+                )
 
         def hidden(t, first, last):
             nc.vector.scalar_tensor_tensor(
                 out=hid_rows[:, t, first:last],
-                in0=sums[t, 1][:, first:last],
+                in0=doubles[t][:, first:last],
                 scalar=unit_quarter[:, t : t + 1],
-                in1=other[t][:, first:last],
+                in1=named[t][:, first:last],
                 op0=ALU.mult,
                 op1=ALU.subtract,
             )
 
-        def last_product(first, last, weave, empty):
+        def last_product(first, last, copy):
             width = last - first
-            hid_bf = work.tile([P, width, PACK], BF16, name="hid_bf", align_bytes=64)
-            weave(
-                out=hid_bf[:].rearrange("p (c i) t -> p c t i", i=4),
-                in_=hid_rows[:, :, first:last].rearrange("p t (c i) -> p c t i", i=4),
-            )
+            hid_woven = work.tile([P, width, PACK], BF16, name="hid_woven", align_bytes=64)
+            weave(copy, hid_woven[:], hid_rows[:, :, first:last])
             hid_codes = work.tile([P, width], U32, name="hid_codes", align_bytes=64)
             hid_scales = work.tile([P, width], U8, name="hid_scales", align_bytes=64)
             nc.vector.quantize_mx(
-                out=hid_codes[:].bitcast(FP8X4), scales=hid_scales[:], in_=hid_bf[:].rearrange("p s t -> p (s t)")
+                out=hid_codes[:].bitcast(FP8X4), scales=hid_scales[:], in_=hid_woven[:].rearrange("p s t -> p (s t)")
             )
-            bank = psum.tile([P, width], F32, name="bank_b", bufs=4)
+            bank = psum.tile([P, width], F32, name="bank_b")
             nc.tensor.matmul_mx(
                 out=bank[:],
                 lhsT=codes["w3"][:].bitcast(FP8X4),
@@ -302,80 +301,53 @@ def tile_picked_ynrtlg_lng_p_kernel(
                 stop=True,
             )
             result = work.tile([P, width], F32, name="result")
-            empty(out=result[:], in_=bank[:])
+            copy(out=result[:], in_=bank[:])
             nc.sync.dma_start(out=out[:, first:last], in_=result[:])
 
         nc.vector.tensor_copy(picked_scales[:], table_scales[:].indirect(offs_sb[:]))
         nc.gpsimd.tensor_scalar(unit_half[:], unit_sb[:], 0.5, 0.0, ALU.mult, ALU.add)
         nc.gpsimd.tensor_scalar(unit_quarter[:], unit_sb[:], 0.25, 0.0, ALU.mult, ALU.add)
-        gather_words(0, 1)
-        cast_weight("w2_00", 0)
-        cast_weight("w2_01", HALF_H)
-        quantize_weight("w2_00")
-        quantize_weight("w2_01")
-        gather_words(1, 2)
-        cast_weight("w2_10", 256)
-        cast_weight("w2_11", 256)
-        quantize_weight("w2_10")
-        quantize_weight("w2_11")
-        cast_weight("w1_0", 192)
-        quantize_weight("w1_0")
-        cast_weight("w1_1", 256)
-        quantize_weight("w1_1")
-        start1(0, 0)
-        start1(0, 1)
-        start1(1, 0)
-        start1(1, 1)
-        product2(0, 0)
-        product2(1, 0)
-        product2(2, 0)
-        product2(3, 0)
-        product2(0, 1)
-        product2(1, 1)
-        product2(2, 1)
-        product2(3, 1)
-        terms1(0, 0)
-        terms1(0, 1)
-        terms1(1, 0)
-        terms1(1, 1)
-        start2(0)
-        start2(1)
-        start2(2)
-        start2(3)
-        share2(0)
-        share2(1)
-        open_first(0)
-        close_first(0)
-        share2(2)
-        open_first(1)
-        close_first(1)
-        excess(0, 0)
-        share2(3)
-        open_first(2)
-        close_first(2)
-        excess(1, 0)
-        open_first(3)
-        close_first(3)
-        excess(2, 0)
-        excess(3, 0)
-        open_second(0)
-        close_second(0)
-        open_second(1)
-        close_second(1)
-        open_second(2)
-        close_second(2)
-        open_second(3)
-        close_second(3)
-        cast_weight("w3", 0)
+        gather_words(0, 0, S)
+        round_weight("w2_00", 0)
+        round_weight("w2_01", HALF_H)
+        for g in range(PASSES):
+            quantize_weight("w2_0%d" % g)
+        gather_words(1, 0, HALF_S)
+        gather_words(1, HALF_S, S)
+        for g in range(PASSES):
+            round_weight("w2_1%d" % g, HALF_H)
+        for g in range(PASSES):
+            quantize_weight("w2_1%d" % g)
+        for g in range(PASSES):
+            round_weight("w1_%d" % g, W1_VECTOR_COLUMNS[g])
+            quantize_weight("w1_%d" % g)
+
+        pieces = [(half, pair) for half in range(2) for pair in range(2)]
+        for half, pair in pieces:
+            bound1(half, pair)
+        for g in range(PASSES):
+            for c in range(CHUNKS):
+                product2(c, g)
+        for half, pair in pieces:
+            terms1(half, pair)
+        for c in range(CHUNKS):
+            bound2(c)
+
+        for step in range(PACK + 2):
+            if step < PACK:
+                composition2(step)
+            if 1 <= step <= PACK:
+                sum_singles(step - 1)
+            if step >= 2:
+                look_up_excess(step - 2)
+        for t in range(PACK):
+            sum_doubles(t)
+        round_weight("w3", 0)
         quantize_weight("w3")
-        hidden(0, 0, 256)
-        hidden(1, 0, 256)
-        hidden(2, 0, 256)
-        hidden(3, 0, 256)
-        hidden(0, 256, S)
-        hidden(1, 256, S)
-        hidden(2, 256, S)
-        hidden(3, 256, S)
-        last_product(0, 256, nc.scalar.copy, nc.scalar.copy)
-        last_product(256, 384, nc.scalar.copy, nc.scalar.copy)
-        last_product(384, S, nc.vector.tensor_copy, nc.vector.tensor_copy)
+
+        for first in (0, HALF_S):
+            for t in range(PACK):
+                hidden(t, first, first + HALF_S)
+        last_product(0, HALF_S, nc.scalar.copy)
+        last_product(HALF_S, HALF_S + P, nc.scalar.copy)
+        last_product(HALF_S + P, S, nc.vector.tensor_copy)

@@ -31,7 +31,7 @@ BANKS = 4
 ALPHA = 0.7
 TINY = 2.0 ** -60
 
-W1_VECTOR_COLUMNS = (192, 256)
+W1_VECTOR_COLUMNS = 256
 SCALAR_COPY_COLUMNS = 128
 
 
@@ -72,10 +72,10 @@ def tile_picked_ynrtlg_lng_p_kernel(
         x1_dealt = x1.rearrange("(p t) s -> p t s", t=PACK)
         for i in range(2):
             nc.sync.dma_start(out=x1_sb[i][:], in_=x1_dealt[:, 2 * i : 2 * i + 2, :])
-        nc.sync.dma_start(out=unit_sb[:], in_=unit.rearrange("(p t) o -> p (t o)", t=PACK))
         load_words(0)
         for g in range(PASSES):
             load_weight("w2_0%d" % g, w2, g, 0, HALF_H)
+        nc.sync.dma_start(out=unit_sb[:], in_=unit.rearrange("(p t) o -> p (t o)", t=PACK))
         load_words(1)
         for g in range(PASSES):
             load_weight("w2_1%d" % g, w2, g, HALF_H, HALF_H)
@@ -184,6 +184,7 @@ def tile_picked_ynrtlg_lng_p_kernel(
         single1 = turned_tile("single1")
         double1 = turned_tile("double1")
         tau1 = {}
+        centred1 = {}
 
         def bound1(half, pair):
             bank = psum.tile([P, S], F32, name="bank_a")
@@ -202,11 +203,13 @@ def tile_picked_ynrtlg_lng_p_kernel(
                 out=tau1[half, pair][:], in_=bank[:].rearrange("r (c p t) -> r c t p", c=2, t=PACK), func=ACT.Tanh
             )
 
-        def terms1(half, pair):
+        def make_single1(half, pair):
             factor = tau1[half, pair][:].rearrange("r c t p -> r (c t) p")
-            centred = composition(factor, by_piece(odds, half, pair), "centred1")
-            times_twice_a(by_piece(single1, half, pair), centred, factor)
-            times_twice_a(by_piece(double1, half, pair), centred, by_piece(single1, half, pair))
+            centred1[half, pair] = composition(factor, by_piece(odds, half, pair), "centred1")
+            times_twice_a(by_piece(single1, half, pair), centred1[half, pair], factor)
+
+        def make_double1(half, pair):
+            times_twice_a(by_piece(double1, half, pair), centred1[half, pair], by_piece(single1, half, pair))
 
         minus_tanh2 = turned_tile("minus_tanh2")
         banks2 = {}
@@ -319,7 +322,7 @@ def tile_picked_ynrtlg_lng_p_kernel(
         for g in range(PASSES):
             quantize_weight("w2_1%d" % g)
         for g in range(PASSES):
-            round_weight("w1_%d" % g, W1_VECTOR_COLUMNS[g])
+            round_weight("w1_%d" % g, W1_VECTOR_COLUMNS)
             quantize_weight("w1_%d" % g)
 
         pieces = [(half, pair) for half in range(2) for pair in range(2)]
@@ -329,7 +332,9 @@ def tile_picked_ynrtlg_lng_p_kernel(
             for c in range(CHUNKS):
                 product2(c, g)
         for half, pair in pieces:
-            terms1(half, pair)
+            make_single1(half, pair)
+        for half, pair in pieces:
+            make_double1(half, pair)
         for c in range(CHUNKS):
             bound2(c)
 

from contextlib import ExitStack

import concourse.mybir as mybir
from concourse.masks import make_identity

K, T, S, N, H = 1024, 2048, 512, 128, 512
FLOPS = 2 * 2 * K * H * S + 2 * H * N * S

F32 = mybir.dt.float32
BF16 = mybir.dt.bfloat16
I32 = mybir.dt.int32
U32 = mybir.dt.uint32
U16 = mybir.dt.uint16
U8 = mybir.dt.uint8
FP8X4 = mybir.dt.float8_e4m3fn_x4
ACT = mybir.ActivationFunctionType
ALU = mybir.AluOpType

P = 128
PACK = 4
PASSES = K // (P * PACK)
CHUNKS = S // P
QUADRANTS = 4
SCALE_ROWS = 4
LIST_ROWS = 16
HALF_S = S // 2
HALF_H = H // 2
HALF_P = P // 2
LINE = 4
BANKS = 4
ALPHA = 0.7
TINY = 2.0 ** -60

W1_VECTOR_COLUMNS = 256
SCALAR_COPY_COLUMNS = 128


def tile_picked_ynrtlg_lng_p_kernel(
    tc, x_words, x_scales, w1, w2, x1, unit, w3, offs, cmp, out
):
    nc = tc.nc
    with ExitStack() as ctx:
        keep = ctx.enter_context(tc.tile_pool(name="keep", bufs=1))
        work = ctx.enter_context(tc.tile_pool(name="work", bufs=4))
        psum = ctx.enter_context(tc.psum_pool(name="psum", bufs=BANKS))

        offs_sb = keep.tile([P, S // LIST_ROWS], U16, name="offs_sb")
        cmp_sb = keep.tile([P, S // LIST_ROWS], U16, name="cmp_sb")
        x1_sb = [keep.tile([P, 2, S], F32, name="x1_%d" % i) for i in range(2)]
        table_scales = keep.tile([P, T], U8, name="table_scales", align_bytes=64)
        table_words = [keep.tile([P, T], I32, name="table_words%d" % g, align_bytes=64) for g in range(PASSES)]
        unit_sb = keep.tile([P, PACK], F32, name="unit_sb")
        ident = keep.tile([P, P], F32, name="ident")
        raw = {}

        def load_weight(key, w, g, first, width):
            raw[key] = keep.tile([P, PACK, width], F32, name="raw_" + key)
            rows = w[g * P * PACK : (g + 1) * P * PACK, first : first + width]
            nc.sync.dma_start(out=raw[key][:], in_=rows.rearrange("(p j) h -> p j h", j=PACK))

        def load_words(g):
            nc.sync.dma_start(out=table_words[g][:], in_=x_words[g].rearrange("p n t -> p (n t)").bitcast(I32))

        nc.vector.memset(table_scales[:].bitcast(I32), 0)
        make_identity(nc, ident[:])
        nc.sync.dma_start(offs_sb[:], offs)
        for q in range(QUADRANTS):
            nc.sync.dma_start(
                out=table_scales[32 * q : 32 * q + SCALE_ROWS * PASSES, :].bitcast(I32),
                in_=x_scales[:, SCALE_ROWS * q : SCALE_ROWS * (q + 1), :].bitcast(I32),
            )
        x1_dealt = x1.rearrange("(p t) s -> p t s", t=PACK)
        for i in range(2):
            nc.sync.dma_start(out=x1_sb[i][:], in_=x1_dealt[:, 2 * i : 2 * i + 2, :])
        load_words(0)
        for g in range(PASSES):
            load_weight("w2_0%d" % g, w2, g, 0, HALF_H)
        nc.sync.dma_start(out=unit_sb[:], in_=unit.rearrange("(p t) o -> p (t o)", t=PACK))
        load_words(1)
        for g in range(PASSES):
            load_weight("w2_1%d" % g, w2, g, HALF_H, HALF_H)
        for g in range(PASSES):
            load_weight("w1_%d" % g, w1, g, 0, H)
        nc.sync.dma_start(cmp_sb[:], cmp)
        load_weight("w3", w3, 0, 0, N)

        def x1_rows(t):
            return x1_sb[t // 2][:, t % 2, :]

        def turned_tile(name):
            return keep.tile([P, CHUNKS, PACK, P], F32, name=name)

        def by_slot(tile, t):
            return tile[:, :, t, :]

        def by_piece(tile, half, pair):
            runs = tile[:].rearrange("r c t p -> r (c t) p")
            return runs[:, 2 * PACK * pair : 2 * PACK * (pair + 1), half * HALF_P : (half + 1) * HALF_P]

        odds = turned_tile("odds")
        for t in range(PACK):
            bank = psum.tile([P, CHUNKS, P], F32, name="bank_a")
            for c in range(CHUNKS):
                nc.tensor.transpose(bank[:, c, :], x1_rows(t)[:, c * P : (c + 1) * P], ident[:])
            ln1 = work.tile([P, CHUNKS, P], F32, name="ln1", bufs=3)
            ln2 = work.tile([P, CHUNKS, P], F32, name="ln2", bufs=3)
            nc.scalar.activation(out=ln1[:], in_=bank[:], func=ACT.Ln, bias=TINY)
            nc.scalar.activation(out=ln2[:], in_=bank[:], func=ACT.Ln, scale=-1.0, bias=1.0)
            nc.vector.tensor_tensor(out=by_slot(odds, t), in0=ln1[:], in1=ln2[:], op=ALU.subtract)

        picked_scales = keep.tile([P, S], U8, name="picked_scales", align_bytes=64)
        picked_words = [keep.tile([P, S], U32, name="picked_words%d" % g, align_bytes=64) for g in range(PASSES)]

        def gather_words(g, first, last):
            nc.vector.tensor_copy(
                picked_words[g][:, first:last],
                table_words[g][:].bitcast(U32).indirect(offs_sb[:, first // LIST_ROWS : last // LIST_ROWS]),
            )

        def weave(copy, woven, rows):
            copy(
                out=woven.rearrange("p (m i) j -> p m j i", i=LINE),
                in_=rows.rearrange("p j (m i) -> p m j i", i=LINE),
            )

        rounded = {}
        codes = {}
        scales = {}

        def round_weight(key, vector_columns):
            width = raw[key].shape[2]
            rounded[key] = keep.tile([P, width, PACK], BF16, name="bf_" + key, align_bytes=64)
            shares = [(nc.vector.tensor_copy, 0, vector_columns)] if vector_columns > 0 else []
            for first in range(vector_columns, width, SCALAR_COPY_COLUMNS):
                shares.append((nc.scalar.copy, first, min(first + SCALAR_COPY_COLUMNS, width)))
            for copy, first, last in shares:
                weave(copy, rounded[key][:, first:last, :], raw[key][:, :, first:last])

        def quantize_weight(key):
            width = raw[key].shape[2]
            codes[key] = keep.tile([P, width], U32, name="codes_" + key, align_bytes=64)
            scales[key] = keep.tile([P, width], U8, name="scales_" + key, align_bytes=64)
            nc.vector.quantize_mx(
                out=codes[key][:].bitcast(FP8X4),
                scales=scales[key][:],
                in_=rounded[key][:].rearrange("p h j -> p (h j)"),
            )

        def picked_product(dst, c, g, key, start, stop):
            cols = slice(c * P, (c + 1) * P)
            nc.tensor.matmul_mx(
                out=dst,
                lhsT=picked_words[g][:, cols].bitcast(FP8X4),
                lhsT_scale=picked_scales[SCALE_ROWS * g : P, cols],
                rhs=codes[key][:].bitcast(FP8X4),
                rhs_scale=scales[key][:],
                start=start,
                stop=stop,
            )

        def composition(bounded, piece_odds, tag):
            z = work.tile(piece_odds.shape, F32, name="z")
            nc.vector.scalar_tensor_tensor(
                out=z[:], in0=bounded, scalar=ALPHA, in1=piece_odds, op0=ALU.mult, op1=ALU.add
            )
            centred = work.tile(piece_odds.shape, F32, name=tag)
            nc.scalar.activation(out=centred[:], in_=z[:], func=ACT.Tanh, scale=-0.5)
            return centred

        def times_twice_a(dst, centred, factor):
            nc.vector.scalar_tensor_tensor(out=dst, in0=centred[:], scalar=1.0, in1=factor, op0=ALU.add, op1=ALU.mult)

        def turn_back(bank, blocks, opens):
            for c in range(CHUNKS):
                nc.tensor.matmul(
                    bank[:, c * P : (c + 1) * P],
                    blocks[:, c, :],
                    ident[:],
                    start=(opens and c == 0),
                    stop=(not opens and c == CHUNKS - 1),
                    is_transpose=True,
                )

        single1 = turned_tile("single1")
        double1 = turned_tile("double1")
        tau1 = {}
        centred1 = {}

        def bound1(half, pair):
            bank = psum.tile([P, S], F32, name="bank_a")
            for g in range(PASSES):
                for i in range(2):
                    picked_product(
                        bank[:, i * HALF_H : (i + 1) * HALF_H],
                        2 * pair + i,
                        g,
                        "w2_%d%d" % (half, g),
                        start=(g == 0 and i == 0),
                        stop=(g == PASSES - 1 and i == 1),
                    )
            tau1[half, pair] = work.tile([P, 2, PACK, HALF_P], F32, name="tau1")
            nc.scalar.activation(
                out=tau1[half, pair][:], in_=bank[:].rearrange("r (c p t) -> r c t p", c=2, t=PACK), func=ACT.Tanh
            )

        def make_single1(half, pair):
            factor = tau1[half, pair][:].rearrange("r c t p -> r (c t) p")
            centred1[half, pair] = composition(factor, by_piece(odds, half, pair), "centred1")
            times_twice_a(by_piece(single1, half, pair), centred1[half, pair], factor)

        def make_double1(half, pair):
            times_twice_a(by_piece(double1, half, pair), centred1[half, pair], by_piece(single1, half, pair))

        minus_tanh2 = turned_tile("minus_tanh2")
        banks2 = {}

        def product2(c, g):
            if g == 0:
                banks2[c] = psum.tile([P, H], F32, name="bank_a")
            picked_product(banks2[c][:], c, g, "w1_%d" % g, start=(g == 0), stop=(g == PASSES - 1))

        def bound2(c):
            nc.scalar.activation(
                out=minus_tanh2[:, c],
                in_=banks2[c][:].rearrange("r (p t) -> r t p", t=PACK),
                func=ACT.Tanh,
                scale=-1.0,
            )

        unit_half = keep.tile([P, PACK], F32, name="unit_half")
        unit_quarter = keep.tile([P, PACK], F32, name="unit_quarter")
        hid_rows = keep.tile([P, PACK, S], BF16, name="hid_rows")
        centred2 = {}
        gam2 = {}
        single2 = {}
        singles = {}
        doubles = {}
        named = {}

        def composition2(t):
            gam2[t] = work.tile([P, CHUNKS, P], F32, name="gam2")
            nc.scalar.activation(out=gam2[t][:], in_=by_slot(minus_tanh2, t), func=ACT.Exp, scale=ALPHA)
            centred2[t] = composition(by_slot(minus_tanh2, t), by_slot(odds, t), "centred2")

        def sum_singles(t):
            singles[t] = psum.tile([P, S], F32, name="bank_b")
            turn_back(singles[t], by_slot(single1, t), True)
            single2[t] = work.tile([P, CHUNKS, P], F32, name="single2")
            times_twice_a(single2[t][:], centred2[t], gam2[t][:])
            turn_back(singles[t], single2[t][:], False)

        def sum_doubles(t):
            doubles[t] = psum.tile([P, S], F32, name="bank_a")
            turn_back(doubles[t], by_slot(double1, t), True)
            double2 = work.tile([P, CHUNKS, P], F32, name="double2")
            times_twice_a(double2[:], centred2[t], single2[t][:])
            turn_back(doubles[t], double2[:], False)

        def look_up_excess(t):
            excess = work.tile([P, S], F32, name="excess")
            nc.vector.scalar_tensor_tensor(
                out=excess[:],
                in0=singles[t][:],
                scalar=unit_half[:, t : t + 1],
                in1=x1_rows(t),
                op0=ALU.mult,
                op1=ALU.mult,
            )
            named[t] = work.tile([P, S], F32, name="named")
            for first in (0, HALF_S):
                nc.scalar.activation(
                    out=named[t][:, first : first + HALF_S],
                    in_=excess[:].indirect(cmp_sb[:, first // LIST_ROWS : (first + HALF_S) // LIST_ROWS]),
                    func=ACT.Copy,
                )

        def hidden(t, first, last):
            nc.vector.scalar_tensor_tensor(
                out=hid_rows[:, t, first:last],
                in0=doubles[t][:, first:last],
                scalar=unit_quarter[:, t : t + 1],
                in1=named[t][:, first:last],
                op0=ALU.mult,
                op1=ALU.subtract,
            )

        def last_product(first, last, copy):
            width = last - first
            hid_woven = work.tile([P, width, PACK], BF16, name="hid_woven", align_bytes=64)
            weave(copy, hid_woven[:], hid_rows[:, :, first:last])
            hid_codes = work.tile([P, width], U32, name="hid_codes", align_bytes=64)
            hid_scales = work.tile([P, width], U8, name="hid_scales", align_bytes=64)
            nc.vector.quantize_mx(
                out=hid_codes[:].bitcast(FP8X4), scales=hid_scales[:], in_=hid_woven[:].rearrange("p s t -> p (s t)")
            )
            bank = psum.tile([P, width], F32, name="bank_b")
            nc.tensor.matmul_mx(
                out=bank[:],
                lhsT=codes["w3"][:].bitcast(FP8X4),
                lhsT_scale=scales["w3"][:],
                rhs=hid_codes[:].bitcast(FP8X4),
                rhs_scale=hid_scales[:],
                start=True,
                stop=True,
            )
            result = work.tile([P, width], F32, name="result")
            copy(out=result[:], in_=bank[:])
            nc.sync.dma_start(out=out[:, first:last], in_=result[:])

        nc.vector.tensor_copy(picked_scales[:], table_scales[:].indirect(offs_sb[:]))
        nc.gpsimd.tensor_scalar(unit_half[:], unit_sb[:], 0.5, 0.0, ALU.mult, ALU.add)
        nc.gpsimd.tensor_scalar(unit_quarter[:], unit_sb[:], 0.25, 0.0, ALU.mult, ALU.add)
        gather_words(0, 0, S)
        round_weight("w2_00", 0)
        round_weight("w2_01", HALF_H)
        for g in range(PASSES):
            quantize_weight("w2_0%d" % g)
        gather_words(1, 0, HALF_S)
        gather_words(1, HALF_S, S)
        for g in range(PASSES):
            round_weight("w2_1%d" % g, HALF_H)
        for g in range(PASSES):
            quantize_weight("w2_1%d" % g)
        for g in range(PASSES):
            round_weight("w1_%d" % g, W1_VECTOR_COLUMNS)
            quantize_weight("w1_%d" % g)

        pieces = [(half, pair) for half in range(2) for pair in range(2)]
        for half, pair in pieces:
            bound1(half, pair)
        for g in range(PASSES):
            for c in range(CHUNKS):
                product2(c, g)
        for half, pair in pieces:
            make_single1(half, pair)
        for half, pair in pieces:
            make_double1(half, pair)
        for c in range(CHUNKS):
            bound2(c)

        for step in range(PACK + 2):
            if step < PACK:
                composition2(step)
            if 1 <= step <= PACK:
                sum_singles(step - 1)
            if step >= 2:
                look_up_excess(step - 2)
        for t in range(PACK):
            sum_doubles(t)
        round_weight("w3", 0)
        quantize_weight("w3")

        for first in (0, HALF_S):
            for t in range(PACK):
                hidden(t, first, first + HALF_S)
        last_product(0, HALF_S, nc.scalar.copy)
        last_product(HALF_S, HALF_S + P, nc.scalar.copy)
        last_product(HALF_S + P, S, nc.vector.tensor_copy)
